import numpy as np, ml_dtypes
CORES = [40,64,80,88,96,104,120,144]
N = 8
import mx_ref
BF = ml_dtypes.bfloat16
def gentries(a):
    return np.ascontiguousarray(a.reshape(8, 16, -1).transpose(0, 2, 1)).reshape(8, -1)
def gtable(e):
    e = np.asarray(e); return np.ascontiguousarray(e.reshape(8, -1, 16).transpose(0, 2, 1)).reshape(128, -1).astype(np.int32)
def gcols(t, e):
    v = np.concatenate([t.reshape(8, 16, -1, 4), np.zeros((8, 16, 1, 4), BF)], axis=2)
    return np.ascontiguousarray(np.stack([v[g][:, e[g]] for g in range(8)])).reshape(128, -1)
def tile(rs):
    return np.stack(rs, axis=2).reshape(128, -1).astype(BF)
def cut(t, i, w=512):
    return t[:, w * i:w * i + w]
def pick(q, e):
    c = np.concatenate([q[0].reshape(128, -1, 4), np.zeros((128, 1, 4), np.uint8)], axis=1); s = np.concatenate([q[1], np.ones((16, 1), np.uint8)], axis=1)
    return (np.ascontiguousarray(c[:, e].reshape(128, -1)), np.ascontiguousarray(s[:, e]))
def join(*qs):
    return (np.concatenate([q[0] for q in qs], axis=1), np.concatenate([q[1] for q in qs], axis=1))
def put(q, e, v):
    c, s = q[0].reshape(128, -1, 4).copy(), q[1].copy(); c[:, e] = v[0].reshape(128, -1, 4); s[:, e] = v[1]
    return (c.reshape(128, -1), s)
def pk(c, s):
    return (np.ascontiguousarray(c), mx_ref.live(s))
def emit(q):
    return q[0], q[1]
def packed(v, rng):
    q = [mx_ref.quantize(np.ascontiguousarray(v[r])) for r in range(N)]
    return np.stack([a for a, b in q]), np.stack([mx_ref.plane(b, rng) for a, b in q])
def values_of_codes():
    e, c = np.zeros((128, 128, 4), np.float32), np.zeros((128, 2, 4), np.uint8)
    e[np.arange(128), np.arange(128), 0] = 1
    c[:127, :, 0] = np.arange(256).reshape(2, 128).T[:127]
    return mx_ref.matmul(mx_ref.quantize(e.reshape(128, 512).astype(BF)), (c.reshape(128, 8), np.full((16, 2), 127, np.uint8))).T.reshape(-1).astype(np.float64)
CODE_VALUE, SCALE_VALUE = values_of_codes(), 2.0 ** (np.arange(256) - 127.0)
def decode(q):
    return (CODE_VALUE[q[0]].reshape(16, 8, -1, 4) * SCALE_VALUE[q[1]][:, None, :, None] + 0.0).reshape(128, -1).astype(np.float32)
def f(rng, *shape):
    return mx_ref.flush((rng.standard_normal(shape, dtype=np.float32) * np.exp2(rng.integers(-2, 3, shape[:-1] + (1,)))).astype(BF))
def wide(rng, *shape, cols=0):
    v = rng.standard_normal(shape, dtype=np.float32) * np.exp2(rng.integers(-12, 13, shape)).astype(np.float32)
    if cols: v *= np.repeat(np.exp2(rng.integers(-cols, cols + 1, shape[:-2] + (1, shape[-1] // 4))) * (rng.random(shape[:-2] + (1, shape[-1] // 4)) > 0.0625), 4, axis=-1).astype(np.float32)
    return mx_ref.flush(v.astype(BF))
C, L, R = 448, 256, 3
def read(pool, at, up):
    a = gcols(pool, at).astype(np.float32)
    b = gcols(pool, np.take_along_axis(up, at, axis=1)).astype(np.float32)
    return mx_ref.quantize(np.ascontiguousarray((a + b).astype(BF)))
def big(v):
    v = v.astype(np.float32)
    v[np.abs(v) < np.float32(2.0 ** -16)] = 0
    return v.astype(BF)
def numbers_of(rng):
    return {"x": big(f(rng, N, 128, 4 * C)), "u": np.array(f(rng, N, 128, 512))}
def listed(p, t):
    return {"par": np.stack([gtable(a) for a in p]), "top": np.stack([gtable(a) for a in t])}
def parents(rng):
    return np.where(rng.random((N, 8, C)) < 0.125, np.arange(C), rng.integers(0, C, (N, 8, C)))
def tops(rng):
    return rng.integers(0, C, (N, 8, L))
def among(rng, k, h):
    o = np.argsort(k, kind="stable")
    return o[rng.integers(np.searchsorted(k[o], h), np.searchsorted(k[o], h, side="right"))]
def weights(rng, w):
    c, p = packed(w, rng)
    return {"wc": c, "ws": p}
def still(rng, k):
    w = np.zeros((N, 128, 4, 128, 4), np.float32)
    i = np.arange(128)
    for b in range(4): w[:, i, b, i, b] = k
    return weights(rng, w.reshape(N, 128, 2048).astype(BF))
def signs(rng):
    return np.stack([rng.permutation(8) % 2 * 2.0 - 1.0 for r in range(N)])
def setup_inputs(rng):
    return {**numbers_of(rng), **listed(parents(rng), tops(rng)), **weights(rng, f(rng, N, 128, 2048))}
def setup_inputs_ties(rng):
    d = numbers_of(rng)
    e = rng.permutation(N)
    x = d["x"].reshape(N, 8, 16, C, 4)
    p, q = parents(rng), tops(rng)
    for r in range(N):
        k, h = (np.zeros(C, int), np.zeros(L, int)) if r == e[0] else (rng.permutation(C) % 3, rng.permutation(L) % 3)
        a = x[r][:, :8, :3].copy()
        a[:, :, 2] = 0
        x[r][:, :8] = a[:, :, k]
        p[r] = among(rng, k, np.tile(k, (8, 1)))
        q[r] = among(rng, k, np.tile(h, (8, 1)))
    x[e[1]] = 0
    u = d["u"].reshape(N, 8, 16, 128, 4)
    u[:, :, 8:, ::16] = 0
    w = np.array(f(rng, N, 128, 2048)).reshape(N, 8, 16, 4, 8, 16, 4)
    w[:, :, :, :, :, :8] = 0
    return {"x": x.reshape(N, 128, 4 * C), "u": u.reshape(N, 128, 512), **listed(p, q), **weights(rng, w.reshape(N, 128, 2048))}
def setup_inputs_near(rng):
    d = numbers_of(rng)
    x = d["x"].astype(np.float32).reshape(N, 8, 16, C, 4)
    m = np.arange(C) // 2
    g = ((m[:, None] >> np.arange(8)) & 1) * np.exp2(np.arange(8) - 23.0)
    a = np.repeat(rng.choice([-0.5, 0.5], (N, 8, C // 2)), 2, axis=-1)
    s = np.repeat(rng.choice([-1.0, 1.0], (N, 8, C // 2)), 2, axis=-1)
    x[:, :, 0] = 0
    x[:, :, 0, :, 0] = a
    x[:, :, 8] = g[:, :4] * s[..., None]
    x[:, :, 9] = g[:, 4:] * s[..., None]
    x[:, :, 10:] = rng.integers(4, 8, (N, 8, 6, C, 4)) * rng.choice([-1.0, 1.0], (N, 8, 6, C, 4)) * 2.0 ** -20
    u = d["u"].reshape(N, 128, 128, 4)
    one = rng.permutation(N) % 2 == 0
    x *= np.where(one, 1.0, 2.0 ** -6).astype(np.float32)[:, None, None, None, None]
    k = np.where(one, 1.0, 2.0 ** -30).astype(np.float32).astype(BF)
    u[:, :, ::16] = 0
    for h in range(0, 128, 16):
        u[:, h, h, 0] = k
        u[:, h + 8:h + 10, h] = k[:, None, None]
    p = np.repeat(rng.integers(0, C, (N, 8, C // 2)), 2, axis=-1)
    q = rng.permuted(np.tile(np.arange(C), (N, 8, 1)), axis=-1)[:, :, :L]
    return {"x": x.reshape(N, 128, 4 * C).astype(BF), "u": u.reshape(N, 128, 512), **listed(p, q), **still(rng, 64)}
def setup_inputs_huge(rng):
    d = numbers_of(rng)
    x = 2.0 ** 28 * (1.25 + 0.5 * rng.random((N, 128, C, 4)))
    one = rng.permutation(N) < N // 2
    p, q = parents(rng), tops(rng)
    for r in range(N):
        k, h = (np.zeros(C, int), np.zeros(L, int)) if one[r] else (rng.permutation(C) % 2, rng.permutation(L) % 2)
        x[r] *= (1.0 - 2.0 * k)[None, :, None]
        p[r] = among(rng, k, np.tile(k, (8, 1)))
        q[r] = among(rng, k, np.tile(h, (8, 1)))
    u = d["u"].reshape(N, 128, 128, 4)
    a = 2.0 ** 30 * (1 - 0.25 * rng.random((N, 128, 8, 4))) * signs(rng)[:, None, :, None]
    u[:, :, ::16] = a.astype(np.float32).astype(BF)
    return {"x": x.astype(np.float32).reshape(N, 128, 4 * C).astype(BF), "u": u.reshape(N, 128, 512), **listed(p, q), **still(rng, 16)}
def setup_inputs_forest(rng):
    d = setup_inputs(rng)
    p, q = parents(rng), tops(rng)
    e = rng.permutation(N)
    p[e[0]] = np.arange(C)
    p[e[1]] = rng.integers(0, C, (8, 1))
    p[e[2]] = (np.arange(C) + 1) % C
    q[e[3]] = rng.integers(0, C, (8, 1))
    return {**d, **listed(p, q)}
def setup_inputs_spread(rng):
    d = setup_inputs(rng)
    d["x"] = big(wide(rng, N, 128, 4 * C, cols=6))
    return d
def check_inputs(d):
    b = []
    for k in ("x", "u"):
        a = np.abs(d[k].astype(np.float32))
        if not (np.isfinite(a).all() and ((a == 0) | (a >= 2.0 ** -30) & (a <= 2.0 ** 30)).all()): b.append("a value of " + k)
    for k in ("par", "top"):
        if not ((d[k] >= 0) & (d[k] < C)).all(): b.append("an entry of " + k)
    return b
def reference(x, u, par, top, wc, ws):
    qu = [mx_ref.quantize(u[r]) for r in range(N)]
    lay = [pk(wc[r], ws[r]) for r in range(N)]
    pool = [x[r] for r in range(N)]
    up = [gentries(par[r]) for r in range(N)]
    at = [gentries(top[r]) for r in range(N)]
    for t in range(R):
        score, sent = [], []
        for r in range(N):
            q = read(pool[r], at[r], up[r])
            score.append(mx_ref.matmul(qu[r], q)[::16] + np.float32(0.0))
            sent.append(mx_ref.quantize(tile([np.maximum(mx_ref.matmul(pick(lay[r], np.arange(128 * b, 128 * b + 128)), q), np.float32(0.0)) * np.float32(0.015625) for b in range(4)])))
        came = decode(join(*sent)).astype(BF)
        for r in range(N):
            n = np.where(score[r] >= 0, C + L * t + np.arange(L), np.take_along_axis(up[r], at[r], axis=1))
            o = np.argsort(-score[r], axis=1, kind="stable")
            pool[r] = np.concatenate([pool[r], cut(came, (r - 1) % N, 4 * L)], axis=1)
            up[r] = np.concatenate([up[r], at[r]], axis=1)
            at[r] = np.take_along_axis(n, o, axis=1)
    y, ol = np.zeros((N, 128, L), np.float32), np.zeros((N, 8, L), np.float32)
    oc, osc = np.zeros((N, 128, 4 * L), np.uint8), np.zeros((N, 16, L), np.uint8)
    for r in range(N):
        q = read(pool[r], at[r], up[r])
        y[r] = mx_ref.matmul(qu[r], q)
        ol[r] = at[r]
        oc[r], osc[r] = emit(q)
    return {"y": y, "ol": ol, "oc": oc, "osc": osc}

@@ -1,0 +1,435 @@
+from concourse.bass import DstId, RemoteDMATransfer
+from concourse.mybir import dt, AluOpType, ActivationFunctionType
+
+C, L, R = 448, 256, 3
+NODES = C + L * R
+OFF = NODES
+B = 2048.0
+NVKS = (6, 10, 10)
+NVA = 0
+QPOS = 3
+NVM, NSM = max(NVKS), 16 - min(NVKS)
+SGW = L + 2
+
+Q4 = "float8_e4m3fn_x4"
+WIDTHS = {
+    "bfloat16": {"pool": 4 * (NODES - L), "sums": 4 * NODES, "xb": 4 * C, "ub": 512, "eb": 2048, "ones": 128, "mm": L, "nm": L, "tt": 4 * L,
+                 "eq": L, "ncr": L, "fl": NVM * L, "so": NVM * 128},
+    "float32": {"sd": C, "tb": OFF + C + 4 * L, "rf": 8, "j4": L, "j16": L, "m4": L, "c4": L, "c16": L, "cw0": 48, "cw": 48, "sa": L, "sb": L,
+                "sc": L, "pt": L, "nf": L, "tw": 16, "prod": L, "ah": L, "na": 16, "sgn": 16, "i1": 16, "i2": 16, "sg": NSM * SGW,
+                "junk": NSM * SGW, "rk": 16, "ys": L},
+    "int32": {"li": 44, "pc": 1, "ri": 3, "uo": 8},
+    "uint16": {"s4": C // 4, "lu": 44, "uu": 8, "t4": 64 * (R + 1), "p4": 64, "iu": 16, "ru": 16},
+    Q4: {"qu": 128, "qr": 128, "wq": 512, "qe": 512},
+    "uint8": {"su": 128, "sr": 128, "wp": 512, "se": 512},
+}
+for _t in range(R + 1):
+    WIDTHS["bfloat16"]["z%d" % _t] = 4 * L
+    WIDTHS[Q4]["qz%d" % _t] = L
+    WIDTHS["uint8"]["sz%d" % _t] = L
+for _t in range(R):
+    WIDTHS["bfloat16"]["h%d" % _t] = 4 * L
+    for _a, _b in (("qh", "sh"), ("rc", "rs"), ("ac", "as")):
+        WIDTHS[Q4]["%s%d" % (_a, _t)] = L
+        WIDTHS["uint8"]["%s%d" % (_b, _t)] = L
+SCRATCH = {_n: ("sbuf", [128, _w], _d) for _d in WIDTHS for _n, _w in WIDTHS[_d].items()}
+for _n, _w in (("psa", 512), ("psb", 512), ("psh", 2048)):
+    SCRATCH[_n] = ("psum", [128, _w], "float32")
+
+POOLS = {"v": 56, "s": 40, "t": 14, "g": 12, "d": 16}
+SEMAPHORES = [q + str(i) for q in POOLS for i in range(POOLS[q])] + ["ls"] + ["ra%d" % t for t in range(R)] + ["aa%d" % t for t in range(R)]
+
+ALU, ACT = AluOpType, ActivationFunctionType
+
+
+def bits(es):
+    m = 0
+    for e in es:
+        m |= 1 << e
+    return m
+
+
+def route(T, topo, r):
+    src, dst = T.cores[r], T.cores[(r + 1) % len(T.cores)]
+    if topo.may_write(src, dst):
+        return None
+    ok = [c for c in topo.cores_of(src) if c != src and topo.may_write(c, dst)]
+    near = [c for c in ok if topo.die(c) == topo.die(src)]
+    far = [c for c in ok if topo.die(c) != topo.die(src)]
+    return [near[0], far[0], near[1]]
+
+
+def relay_program(g, core, T, topo):
+    n = len(T.cores)
+    for r in range(n):
+        way = route(T, topo, r)
+        if way is None or core not in way:
+            continue
+        src, dst = T.cores[r], T.cores[(r + 1) % n]
+        k = way.index(core)
+        on = len(topo.engines(src, core))
+        rid, pid = topo.addr(dst, core)
+        mask = topo.mask(core, dst)
+        for t in range(R):
+            if k < 2:
+                g.wait_ge(T.sem["ra%d" % t], on // 2)
+                a, b = 128 * k, 128 * k + 128
+                g.remote_dma(T["ac%d" % t][:, a:b].bitcast(dt.uint8), T["rc%d" % t][:, a:b].bitcast(dt.uint8),
+                             T.sem["aa%d" % t], T.sem.ls, pid, rid, mask)
+            else:
+                g.wait_ge(T.sem["ra%d" % t], on)
+                g.remote_dma(T["as%d" % t][:], T["rs%d" % t][:], T.sem["aa%d" % t], T.sem.ls, pid, rid, mask)
+        g.wait_ge(T.sem.ls, R * len(topo.engines(core, dst)))
+
+
+def rank_program(g, core, T, topo):
+    rank = T.rank_of(core)
+    if rank is None:
+        relay_program(g, core, T, topo)
+        return
+    n = len(T.cores)
+    nxt, prv = T.cores[(rank + 1) % n], T.cores[(rank - 1) % n]
+    way, back = route(T, topo, rank), route(T, topo, (rank - 1) % n)
+    if back is None:
+        arrive = 2 * len(topo.engines(prv, core))
+    else:
+        arrive = sum(len(topo.engines(c, core)) for c in back)
+    queues = {"v": g.vector, "s": g.scalar, "t": g.tensor, "g": g, "y": g.sync}
+    ops = []
+
+    def V(name, a=None, b=None, s=1):
+        w = T[name].shape[1]
+        a, b = (0 if a is None else a), (w if b is None else b)
+        ap = T[name][:, a:b] if s == 1 else T[name][:, a:b:s]
+        if SCRATCH[name][0] == "psum":
+            return (ap, [(name, 1 << (a // 512))])
+        return (ap, [(name, bits(range(a, b, s)))])
+
+    def pick(win, off):
+        return (win[0].indirect(off[0]), win[1] + off[1])
+
+    def op(q, fn, reads, writes, ext=None, kind="c"):
+        ops.append({"q": q, "fn": fn, "r": [x for v in reads for x in v[1]], "w": [x for v in writes for x in v[1]], "ext": ext, "kind": kind})
+
+    def sc(x):
+        return (x[0], [x]) if isinstance(x, tuple) else (x, [])
+
+    def ts(out, in0, s1, o0, s2=None, o1=None):
+        (a, ra), (b, rb) = sc(s1), sc(s2)
+        if o1 is None:
+            op("v", lambda: g.vector.tensor_scalar(out[0], in0[0], a, None, o0), [in0] + ra, [out])
+        else:
+            op("v", lambda: g.vector.tensor_scalar(out[0], in0[0], a, b, o0, o1), [in0] + ra + rb, [out])
+
+    def tt(out, in0, in1, o):
+        op("v", lambda: g.vector.tensor_tensor(out[0], in0[0], in1[0], o), [in0, in1], [out])
+
+    def cp(out, in_):
+        op("v", lambda: g.vector.tensor_copy(out[0], in_[0]), [in_], [out])
+
+    def scan(out, d0, d1, init, o0, o1):
+        a, ra = sc(init)
+        op("v", lambda: g.vector.tensor_tensor_scan(out[0], d0[0], d1[0], a, o0, o1), [d0, d1] + ra, [out])
+
+    def act(out, in_, f, bias=None, scale=None, acc=None):
+        kw, rd, wr = {}, [in_], [out]
+        if bias is not None:
+            kw["bias"], ra = sc(bias)
+            rd += ra
+        if scale is not None:
+            kw["scale"] = scale
+        if acc is not None:
+            kw["accum_out"] = acc[0]
+            wr.append(acc)
+        op("s", lambda: g.scalar.activation(out[0], in_[0], f, **kw), rd, wr)
+
+    def quant(q, s, in_):
+        op("v", lambda: g.vector.quantize_mx(q[0], s[0], in_[0]), [in_], [q, s])
+
+    def mx(out, lq, ls, rq, rs, ext=None):
+        op("t", lambda: g.tensor.matmul_mx(out[0], lq[0], ls[0], rq[0], rs[0], True, True), [lq, ls, rq, rs], [out], ext)
+
+    def iota(out, pattern, base, cm, fl=True):
+        if fl:
+            op("g", lambda: g.iota(out[0], pattern, base, cm, allow_small_or_imprecise_dtypes=True), [], [out])
+        else:
+            op("g", lambda: g.iota(out[0], pattern, base, cm), [], [out])
+
+    def dma(q, out, in_, reads, writes):
+        op(q, lambda: queues[q].dma_start(out, in_), reads, writes, kind="d")
+
+    def u8(v):
+        return v[0].bitcast(dt.uint8)
+
+    rcol, qcol, tcol, b16, col4, tmpc, negr = [V("rf", i, i + 1) for i in range(7)]
+
+    dma("y", T.li[:, 0:28], T.par[:], [], [V("li", 0, 28)])
+    dma("y", T.li[:, 28:44], T.top[:], [], [V("li", 28, 44)])
+    dma("s", T.pool[:, 0:4 * C], T.x[:], [], [V("pool", 0, 4 * C)])
+    dma("y", T.ub[:], T.u[:], [], [V("ub")])
+    dma("y", u8(V("wq")), T.wc[:], [V("li", 28, 44)], [V("wq")])
+    dma("y", T.wp[:], T.ws[:], [], [V("wp")])
+    dma("y", T.xb[:], T.x[:], [V("wp")], [V("xb")])
+
+    iota(V("pc"), [[0, 1]], 0, 1, False)
+    iota(V("j4"), [[0, 64], [1, 4]], 0, 0)
+    iota(V("tb", 0, C), [[1, C]], 0, 0)
+    iota(V("j16"), [[0, 16], [1, 16]], 0, 0)
+    iota(V("uo"), [[16, 8]], 0, 0, False)
+    op("v", lambda: g.vector.memset(T.ones[:], 1.0), [], [V("ones")])
+    op("v", lambda: g.vector.memset(T.eb[:], 0.0), [], [V("eb")])
+
+    def unit(b):
+        o = V("eb", 512 * b + b, 512 * b + 512, 4)
+        op("g", lambda: g.affine_select(o[0], T.ones[:], [[-1, 128]], ALU.is_equal, 0.0, 0, 1), [V("ones")], [o])
+    for b in range(4):
+        unit(b)
+    iota(V("cw0"), [[16, 48]], C, 0)
+    iota(V("tb", C, NODES), [[1, NODES - C]], C, 0)
+
+    ts(V("ri", 0, 1), V("pc"), 15, ALU.bitwise_and)
+    ts(V("ri", 1, 2), V("pc"), 2, ALU.logical_shift_right, 3, ALU.bitwise_and)
+    ts(V("ri", 2, 3), V("pc"), 3, ALU.bitwise_and)
+    cp(V("rf", 0, 3), V("ri"))
+    ts(V("m4"), V("j4"), qcol, ALU.is_equal)
+    ts(tmpc, qcol, 4 * B, ALU.mult, tcol, ALU.add)
+    ts(V("c4"), V("m4"), -6 * B, ALU.mult, B, ALU.add)
+    cp(V("lu"), V("li"))
+    ts(col4, tmpc, -12 * B, ALU.add)
+
+    def list4(out, src, tmp):
+        scan(V(tmp), V("c4"), src, 0.0, ALU.add, ALU.max)
+        ts(out, V(tmp, 3, L, 4), 4.0, ALU.mult, col4, ALU.add)
+
+    def tops(t):
+        return V("tb", OFF + C + L * t, OFF + C + L * (t + 1))
+
+    def t4(t, a=0, b=64):
+        return V("t4", 64 * t + a, 64 * t + b)
+
+    act(negr, rcol, ACT.Identity, scale=-1.0)
+    act(b16, rcol, ACT.Identity, bias=15 * B, scale=-B)
+    act(V("tb", OFF, OFF + C), pick(V("tb", 0, C), V("lu", 0, 28)), ACT.Copy)
+    cp(tops(0), pick(V("tb", 0, C), V("lu", 28, 44)))
+    act(V("pt"), pick(V("tb", OFF, OFF + C), V("lu", 28, 44)), ACT.Copy)
+    list4(t4(0), tops(0), "sa")
+    quant(V("qu"), V("su"), V("ub"))
+    cp(V("uu"), V("uo"))
+    list4(V("p4"), V("pt"), "sb")
+    op("v", lambda: g.vector.tensor_copy(T.qr[:].bitcast(dt.uint32), T.qu[:].bitcast(dt.uint32).indirect(T.uu[:])), [V("qu"), V("uu")], [V("qr")])
+    for k in range(4):
+        act(V("tt", L * k, L * k + L), pick(V("pool", 0, 4 * C), t4(0, 16 * k, 16 * k + 16)), ACT.Copy)
+    for k in range(4):
+        tt(V("z0", L * k, L * k + L), pick(V("pool", 0, 4 * C), V("p4", 16 * k, 16 * k + 16)), V("tt", L * k, L * k + L), ALU.add)
+    quant(V("qz0"), V("sz0"), V("z0"))
+    act(V("sr"), pick(V("su"), V("uu")), ACT.Copy)
+    act(V("prod"), V("j16"), ACT.Abs, bias=negr)
+    act(V("mm"), V("prod"), ACT.Relu, bias=1.0, scale=-1.0)
+    act(V("nm"), V("prod"), ACT.Sign)
+    sent = [0]
+
+    def send(t):
+        qh, sh = "qh%d" % t, "sh%d" % t
+        if way is None:
+            rid, pid = topo.addr(nxt, core)
+            mask = topo.mask(core, nxt)
+            op("g", lambda: g.remote_dma(u8(V("ac%d" % t)), u8(V(qh)), T.sem["aa%d" % t], T.sem.ls, pid, rid, mask), [V(qh)], [], kind="r")
+            op("g", lambda: g.remote_dma(T["as%d" % t][:], T[sh][:], T.sem["aa%d" % t], T.sem.ls, pid, rid, mask), [V(sh)], [], kind="r")
+            sent[0] += 2 * len(topo.engines(core, nxt))
+            return
+        parts = []
+        for k in range(2):
+            es = topo.engines(core, way[k])[k::2]
+            rid, pid = topo.addr(way[k], core)
+            parts.append(RemoteDMATransfer(dst_ids=[DstId(rid=rid, pnc=pid)], dma_engine_mask=bits(es), remote_sem=T.sem["ra%d" % t],
+                                           src=u8(V(qh, 128 * k, 128 * k + 128)), dst=u8(V("rc%d" % t, 128 * k, 128 * k + 128))))
+            sent[0] += len(es)
+        op("g", lambda: g.remote_dma_fused(parts, local_sem=T.sem.ls), [V(qh)], [], kind="r")
+        rid, pid = topo.addr(way[2], core)
+        mask = topo.mask(core, way[2])
+        op("g", lambda: g.remote_dma(T["rs%d" % t][:], T[sh][:], T.sem["ra%d" % t], T.sem.ls, pid, rid, mask), [V(sh)], [], kind="r")
+        sent[0] += len(topo.engines(core, way[2]))
+
+    for t in range(R):
+        qz, sz, h = V("qz%d" % t), V("sz%d" % t), "h%d" % t
+        sa, sb = V("psa", 0, L), V("psb", 0, L)
+        nvk = NVKS[t]
+        nsk = 16 - nvk
+
+        def bank(b):
+            return V("psh", 512 * b, 512 * b + L)
+
+        def wmx(b):
+            mx(bank(b), V("wq", 128 * b, 128 * b + 128), V("wp", 128 * b, 128 * b + 128), qz, sz)
+        for b in range(1 + NVA):
+            wmx(b)
+        mx(sa, V("qr"), V("sr"), qz, sz)
+        for b in range(1 + NVA, 4):
+            wmx(b)
+        mx(sb, V("qr"), V("sr"), qz, sz)
+        for b in range(4):
+            if 1 <= b <= NVA:
+                ts(V(h, b, 4 * L, 4), bank(b), 0.0, ALU.max, 0.015625, ALU.mult)
+            else:
+                act(V(h, b, 4 * L, 4), bank(b), ACT.Relu, scale=0.015625)
+        steps = [lambda: tt(V("prod"), sa, V("mm"), ALU.mult),
+                 lambda: scan(V("ah"), V("nm"), V("prod"), 0.0, ALU.mult, ALU.add),
+                 lambda: tt(V("eq"), sa, V("ah"), ALU.is_equal),
+                 lambda: scan(V("ncr"), V("nm"), V("eq"), 0.0, ALU.mult, ALU.subtract)]
+        for s in steps[:QPOS]:
+            s()
+        quant(V("qh%d" % t), V("sh%d" % t), V(h))
+        send(t)
+        for s in steps[QPOS:]:
+            s()
+        act(V("na"), V("ah", 15, L, 16), ACT.Identity, scale=-1.0)
+        act(V("sgn"), V("na"), ACT.Sign)
+        if t == 0:
+            ts(V("tw"), V("li", 28, 44), float(OFF), ALU.add)
+            ts(V("cw"), V("cw0"), rcol, ALU.add)
+
+        def vcmp(i):
+            e = 16 * (nsk + i) + 16
+            a = V("ah", e - 1, e)
+            ts(V("fl", L * i, L * i + e), V("psa", 0, e), a, ALU.is_ge)
+            if e < L:
+                ts(V("fl", L * i + e, L * i + L), V("psa", e, L), a, ALU.is_gt)
+
+        def vsum(i):
+            e = 16 * (nsk + i) + 16
+            scan(V("so", 128 * i, 128 * i + 128), V("fl", L * i, L * i + 128), V("fl", L * i + 128, L * i + L), V("ncr", e - 1, e), ALU.add, ALU.add)
+
+        def s1(k):
+            act(V("sg", SGW * k, SGW * k + L), sb, ACT.Sign, bias=V("na", k, k + 1))
+
+        def s2(k):
+            o, e = SGW * k, 16 * k + 16
+            act(V("junk", o, o + e), V("sg", o, o + e), ACT.Sign, bias=1.0, acc=V("sg", o + L, o + L + 1))
+
+        def s3(k):
+            o, e = SGW * k, 16 * k + 16
+            act(V("junk", o + e, o + SGW), V("sg", o + e, o + SGW), ACT.Relu, acc=V("rk", k, k + 1))
+
+        vcmp(0)
+        tt(V("i1"), V("sgn"), V("tw"), ALU.mult)
+        vcmp(1)
+        tt(V("i2"), V("i1"), V("cw", 16 * t, 16 * t + 16), ALU.max)
+        vsum(0)
+        cp(V("iu"), V("i2"))
+        for i in range(2, nvk):
+            vcmp(i)
+            vsum(i - 1)
+        vsum(nvk - 1)
+        for k in range(nsk + 2):
+            if k < nsk:
+                s1(k)
+            if k == 1:
+                act(V("sg", SGW - 1, nsk * SGW, SGW), V("ncr", 15, 16 * nsk, 16), ACT.Identity, bias=16.0)
+            if 1 <= k <= nsk:
+                s2(k - 1)
+            if k == nsk:
+                act(V("nf"), pick(V("tb", 0, OFF + C + L * t), V("iu")), ACT.Copy)
+            if k >= 2:
+                s3(k - 2)
+        ts(V("ru", nsk, 16), V("so", 127, 128 * nvk, 128), 0.0, ALU.add)
+        if t == 0:
+            quant(V("qe"), V("se"), V("eb"))
+            scan(V("sd", 0, L), V("c4"), V("tb", OFF, OFF + L), 0.0, ALU.add, ALU.max)
+            scan(V("sd", L, C), V("c4", 0, C - L), V("tb", OFF + L, OFF + C), 0.0, ALU.add, ALU.max)
+            ts(V("s4"), V("sd", 3, C, 4), 4.0, ALU.mult, col4, ALU.add)
+            tt(V("sums", 0, 4 * C), pick(V("pool", 0, 4 * C), V("s4")), V("xb"), ALU.add)
+            act(V("c16"), V("mm"), ACT.Identity, bias=B, scale=-18 * B)
+        else:
+            act(V("tt"), pick(V("pool", 0, 4 * (C + L * t)), t4(t)), ACT.Copy)
+        ts(V("ru", 0, nsk), V("rk", 0, nsk), -16.0, ALU.add)
+        new = tops(t + 1)
+        op("v", lambda new=new: g.vector.tensor_copy(new[0].indirect(T.ru[:]), T.nf[:]), [V("ru"), V("nf")], [new])
+        if t == R - 1:
+            dma("y", T.ol[:], T.tb[0:128:16, OFF + C + L * R:OFF + C + L * (R + 1)], [new], [])
+        list4(t4(t + 1), new, "sa")
+        order = (0, 3, 1, 2) if t < R - 1 else (0, 1, 2, 3)
+        for b in order:
+            mx(bank(b), V("qe", 128 * b, 128 * b + 128), V("se", 128 * b, 128 * b + 128), V("ac%d" % t), V("as%d" % t),
+               ext=(T.sem["aa%d" % t], arrive) if b == 0 else None)
+        base = 4 * (C + L * t)
+        for b in range(4):
+            if t < R - 1:
+                c = (b + 3) % 4
+                act(V("pool", base + c, base + 4 * L, 4), bank(c), ACT.Copy)
+            tt(V("sums", base + b, base + 4 * L, 4), bank(b), V("tt", b, 4 * L, 4), ALU.add)
+        z, win = "z%d" % (t + 1), V("sums", 0, base + 4 * L)
+        cp(V(z, 0, 2 * L), pick(win, t4(t + 1, 0, 32)))
+        act(V(z, 2 * L, 4 * L), pick(win, t4(t + 1, 32, 64)), ACT.Copy)
+        quant(V("qz%d" % (t + 1)), V("sz%d" % (t + 1)), V(z))
+        if t < R - 1:
+            scan(V("sc"), V("c16"), new, 0.0, ALU.add, ALU.max)
+            ts(V("tw"), V("sc", 15, L, 16), b16, ALU.subtract, float(OFF), ALU.add)
+
+    qz, sz = V("qz%d" % R), V("sz%d" % R)
+    mx(V("psa", 0, L), V("qu"), V("su"), qz, sz)
+    dma("y", T.oc[:], u8(qz), [qz], [])
+    for k in range(4):
+        dma("y" if k < 2 else "s", T.osc[4 * k:4 * k + 4, :], T["sz%d" % R][32 * k:32 * k + 4, :], [sz], [])
+    cp(V("ys"), V("psa", 0, L))
+    dma("s", T.y[:], T.ys[:], [V("ys")], [])
+
+    hist, known, at, waits = {}, {q: set() for q in queues}, [], []
+    for i, o in enumerate(ops):
+        deps = set()
+        accs = [(x, False) for x in o["r"]] + [(x, True) for x in o["w"]]
+        for acc, wr in accs:
+            psum = SCRATCH[acc[0]][0] == "psum"
+            for j, m, w in hist.get(acc[0], []):
+                if m & acc[1] and (w or wr or (psum and ops[j]["q"] != o["q"])):
+                    deps.add(j)
+        mine = []
+        for j in sorted(deps, reverse=True):
+            if j not in known[o["q"]]:
+                mine.append(j)
+                known[o["q"]] |= at[j] | {j}
+        waits.append(mine)
+        at.append(set(known[o["q"]]))
+        for acc, wr in accs:
+            hist.setdefault(acc[0], []).append((i, acc[1], wr))
+    waiters = {}
+    for i, w in enumerate(waits):
+        for j in w:
+            waiters.setdefault(j, []).append(i)
+    group = {}
+    for j, w in waiters.items():
+        group[j] = (ops[j]["q"], tuple(w)) if ops[j]["kind"] == "c" else ("own", j)
+    members = {}
+    for j in sorted(group):
+        members.setdefault(group[j], []).append(j)
+    used, last, count, mark = {q: 0 for q in POOLS}, {}, {}, {}
+    for i, o in enumerate(ops):
+        q = queues[o["q"]]
+        done = []
+        for j in waits[i]:
+            if group[j] not in done:
+                done.append(group[j])
+                q.wait_ge(*mark[group[j]])
+        if o["ext"] is not None:
+            q.wait_ge(*o["ext"])
+        if o["kind"] == "d":
+            name = "d%d" % used["d"]
+            used["d"] += 1
+            mark[("own", i)] = (T.sem[name], 16)
+            o["fn"]().then_inc(T.sem[name], 16)
+        elif i in group:
+            k = group[i]
+            if k not in mark:
+                name = o["q"] + str(used[o["q"]] % POOLS[o["q"]])
+                used[o["q"]] += 1
+                if name in last and any(j not in at[i] for j in members[last[name]]):
+                    q.wait_ge(*mark[last[name]])
+                last[name] = k
+                count[name] = count.get(name, 0) + len(members[k])
+                mark[k] = (T.sem[name], count[name])
+            o["fn"]().then_inc(mark[k][0], 1)
+        else:
+            o["fn"]()
+    for i, o in enumerate(ops):
+        if o["kind"] == "d" and i not in group:
+            queues[o["q"]].wait_ge(*mark[("own", i)])
+    g.wait_ge(T.sem.ls, sent[0])

@@ -3,23 +3,25 @@ from concourse.mybir import dt, AluOpType, ActivationFunctionType
 
 C, L, R = 448, 256, 3
 NODES = C + L * R
+PW = NODES - L
 OFF = NODES
 B = 2048.0
-NVKS = (6, 10, 10)
-NVA = 0
-QPOS = 3
+NVKS = (10, 10, 10)
+PRE = (4, 1, 1)
+NVAS = (1, 0, 0)
+QPOSS = (0, 3, 3)
 NVM, NSM = max(NVKS), 16 - min(NVKS)
 SGW = L + 2
 
 Q4 = "float8_e4m3fn_x4"
 WIDTHS = {
-    "bfloat16": {"pool": 4 * (NODES - L), "sums": 4 * NODES, "xb": 4 * C, "ub": 512, "eb": 2048, "ones": 128, "mm": L, "nm": L, "tt": 4 * L,
+    "bfloat16": {"pool": 4 * PW, "sums": 4 * NODES, "xs": 4 * C, "ub": 512, "eb": 2048, "ones": 128, "mm": L, "nm": L, "tt": 4 * L,
                  "eq": L, "ncr": L, "fl": NVM * L, "so": NVM * 128},
-    "float32": {"sd": C, "tb": OFF + C + 4 * L, "rf": 8, "j4": L, "j16": L, "m4": L, "c4": L, "c16": L, "cw0": 48, "cw": 48, "sa": L, "sb": L,
-                "sc": L, "pt": L, "nf": L, "tw": 16, "prod": L, "ah": L, "na": 16, "sgn": 16, "i1": 16, "i2": 16, "sg": NSM * SGW,
+    "float32": {"tb": OFF + C + 4 * L, "rf": 8, "j16": L, "c16": L, "cw0": 48, "cw": 48,
+                "sc": L, "nf": L, "tw": 16, "prod": L, "ah": L, "na": 16, "sgn": 16, "i1": 16, "i2": 16, "sg": NSM * SGW,
                 "junk": NSM * SGW, "rk": 16, "ys": L},
-    "int32": {"li": 44, "pc": 1, "ri": 3, "uo": 8},
-    "uint16": {"s4": C // 4, "lu": 44, "uu": 8, "t4": 64 * (R + 1), "p4": 64, "iu": 16, "ru": 16},
+    "int32": {"li": 44, "pc": 1, "ri": 1, "uo": 8},
+    "uint16": {"lu": 44, "uu": 8, "tl": 16 * R, "iu": 16, "ru": 16},
     Q4: {"qu": 128, "qr": 128, "wq": 512, "qe": 512},
     "uint8": {"su": 128, "sr": 128, "wp": 512, "se": 512},
 }
@@ -161,19 +163,16 @@ def rank_program(g, core, T, topo):
     def u8(v):
         return v[0].bitcast(dt.uint8)
 
-    rcol, qcol, tcol, b16, col4, tmpc, negr = [V("rf", i, i + 1) for i in range(7)]
+    rcol, b16, negr = [V("rf", i, i + 1) for i in range(3)]
 
     dma("y", T.li[:, 0:28], T.par[:], [], [V("li", 0, 28)])
     dma("y", T.li[:, 28:44], T.top[:], [], [V("li", 28, 44)])
-    dma("s", T.pool[:, 0:4 * C], T.x[:], [], [V("pool", 0, 4 * C)])
-    dma("y", T.ub[:], T.u[:], [], [V("ub")])
+    dma("s", T.xs[:], T.x[:], [], [V("xs")])
     dma("y", u8(V("wq")), T.wc[:], [V("li", 28, 44)], [V("wq")])
     dma("y", T.wp[:], T.ws[:], [], [V("wp")])
-    dma("y", T.xb[:], T.x[:], [V("wp")], [V("xb")])
+    dma("y", T.ub[:], T.u[:], [], [V("ub")])
 
     iota(V("pc"), [[0, 1]], 0, 1, False)
-    iota(V("j4"), [[0, 64], [1, 4]], 0, 0)
-    iota(V("tb", 0, C), [[1, C]], 0, 0)
     iota(V("j16"), [[0, 16], [1, 16]], 0, 0)
     iota(V("uo"), [[16, 8]], 0, 0, False)
     op("v", lambda: g.vector.memset(T.ones[:], 1.0), [], [V("ones")])
@@ -182,50 +181,55 @@ def rank_program(g, core, T, topo):
     def unit(b):
         o = V("eb", 512 * b + b, 512 * b + 512, 4)
         op("g", lambda: g.affine_select(o[0], T.ones[:], [[-1, 128]], ALU.is_equal, 0.0, 0, 1), [V("ones")], [o])
+    iota(V("tb", 0, C), [[1, C]], 0, 0)
     for b in range(4):
         unit(b)
     iota(V("cw0"), [[16, 48]], C, 0)
     iota(V("tb", C, NODES), [[1, NODES - C]], C, 0)
 
-    ts(V("ri", 0, 1), V("pc"), 15, ALU.bitwise_and)
-    ts(V("ri", 1, 2), V("pc"), 2, ALU.logical_shift_right, 3, ALU.bitwise_and)
-    ts(V("ri", 2, 3), V("pc"), 3, ALU.bitwise_and)
-    cp(V("rf", 0, 3), V("ri"))
-    ts(V("m4"), V("j4"), qcol, ALU.is_equal)
-    ts(tmpc, qcol, 4 * B, ALU.mult, tcol, ALU.add)
-    ts(V("c4"), V("m4"), -6 * B, ALU.mult, B, ALU.add)
-    cp(V("lu"), V("li"))
-    ts(col4, tmpc, -12 * B, ALU.add)
-
-    def list4(out, src, tmp):
-        scan(V(tmp), V("c4"), src, 0.0, ALU.add, ALU.max)
-        ts(out, V(tmp, 3, L, 4), 4.0, ALU.mult, col4, ALU.add)
+    ts(V("ri"), V("pc"), 15, ALU.bitwise_and)
+    cp(rcol, V("ri"))
+    cp(V("uu"), V("uo"))
+    act(negr, rcol, ACT.Identity, scale=-1.0)
+    act(b16, rcol, ACT.Identity, bias=15 * B, scale=-B)
+    act(V("prod"), V("j16"), ACT.Abs, bias=negr)
+    act(V("mm"), V("prod"), ACT.Relu, bias=1.0, scale=-1.0)
 
     def tops(t):
         return V("tb", OFF + C + L * t, OFF + C + L * (t + 1))
 
-    def t4(t, a=0, b=64):
-        return V("t4", 64 * t + a, 64 * t + b)
+    def tl(t, a=0, b=16):
+        return V("lu", 28 + a, 28 + b) if t == 0 else V("tl", 16 * (t - 1) + a, 16 * (t - 1) + b)
 
-    act(negr, rcol, ACT.Identity, scale=-1.0)
-    act(b16, rcol, ACT.Identity, bias=15 * B, scale=-B)
-    act(V("tb", OFF, OFF + C), pick(V("tb", 0, C), V("lu", 0, 28)), ACT.Copy)
-    cp(tops(0), pick(V("tb", 0, C), V("lu", 28, 44)))
-    act(V("pt"), pick(V("tb", OFF, OFF + C), V("lu", 28, 44)), ACT.Copy)
-    list4(t4(0), tops(0), "sa")
-    quant(V("qu"), V("su"), V("ub"))
-    cp(V("uu"), V("uo"))
-    list4(V("p4"), V("pt"), "sb")
-    op("v", lambda: g.vector.tensor_copy(T.qr[:].bitcast(dt.uint32), T.qu[:].bitcast(dt.uint32).indirect(T.uu[:])), [V("qu"), V("uu")], [V("qr")])
-    for k in range(4):
-        act(V("tt", L * k, L * k + L), pick(V("pool", 0, 4 * C), t4(0, 16 * k, 16 * k + 16)), ACT.Copy)
-    for k in range(4):
-        tt(V("z0", L * k, L * k + L), pick(V("pool", 0, 4 * C), V("p4", 16 * k, 16 * k + 16)), V("tt", L * k, L * k + L), ALU.add)
+    def plane(name, b, lo, hi):
+        w = PW if name == "pool" else NODES
+        return V(name, w * b + lo, w * b + hi)
+
+    def read(t, b, eng, a=0, e=16):
+        o, i = V("z%d" % t, 64 * a + b, 64 * e, 4), pick(plane("sums", b, 0, C + L * t), tl(t, a, e))
+        if eng == "v":
+            cp(o, i)
+        else:
+            act(o, i, ACT.Copy)
+
+    cp(plane("pool", 0, 0, C), V("xs", 0, 4 * C, 4))
+    cp(V("lu"), V("li"))
+    for b in range(1, 4):
+        act(plane("pool", b, 0, C), V("xs", b, 4 * C, 4), ACT.Copy)
+    for b in range(4):
+        tt(plane("sums", b, 0, C), pick(plane("pool", b, 0, C), V("lu", 0, 28)), V("xs", b, 4 * C, 4), ALU.add)
+        if b < 3:
+            read(0, b, "s")
+        if b == 1:
+            act(V("nm"), V("prod"), ACT.Sign)
+        if b == 2:
+            act(V("c16"), V("mm"), ACT.Identity, bias=B, scale=-18 * B)
+    read(0, 3, "v", 0, 8)
+    read(0, 3, "s", 8, 16)
     quant(V("qz0"), V("sz0"), V("z0"))
-    act(V("sr"), pick(V("su"), V("uu")), ACT.Copy)
-    act(V("prod"), V("j16"), ACT.Abs, bias=negr)
-    act(V("mm"), V("prod"), ACT.Relu, bias=1.0, scale=-1.0)
-    act(V("nm"), V("prod"), ACT.Sign)
+    quant(V("qu"), V("su"), V("ub"))
+    op("v", lambda: g.vector.tensor_copy(T.qr[:].bitcast(dt.uint32), T.qu[:].bitcast(dt.uint32).indirect(T.uu[:])), [V("qu"), V("uu")], [V("qr")])
+    cp(V("sr"), pick(V("su"), V("uu")))
     sent = [0]
 
     def send(t):
@@ -261,14 +265,14 @@ def rank_program(g, core, T, topo):
 
         def wmx(b):
             mx(bank(b), V("wq", 128 * b, 128 * b + 128), V("wp", 128 * b, 128 * b + 128), qz, sz)
-        for b in range(1 + NVA):
+        for b in range(PRE[t]):
             wmx(b)
         mx(sa, V("qr"), V("sr"), qz, sz)
-        for b in range(1 + NVA, 4):
+        for b in range(PRE[t], 4):
             wmx(b)
         mx(sb, V("qr"), V("sr"), qz, sz)
         for b in range(4):
-            if 1 <= b <= NVA:
+            if b >= 4 - NVAS[t]:
                 ts(V(h, b, 4 * L, 4), bank(b), 0.0, ALU.max, 0.015625, ALU.mult)
             else:
                 act(V(h, b, 4 * L, 4), bank(b), ACT.Relu, scale=0.015625)
@@ -276,11 +280,13 @@ def rank_program(g, core, T, topo):
                  lambda: scan(V("ah"), V("nm"), V("prod"), 0.0, ALU.mult, ALU.add),
                  lambda: tt(V("eq"), sa, V("ah"), ALU.is_equal),
                  lambda: scan(V("ncr"), V("nm"), V("eq"), 0.0, ALU.mult, ALU.subtract)]
-        for s in steps[:QPOS]:
+        for s in steps[:QPOSS[t]]:
             s()
         quant(V("qh%d" % t), V("sh%d" % t), V(h))
         send(t)
-        for s in steps[QPOS:]:
+        if t == 0:
+            act(V("tb", OFF, OFF + C), pick(V("tb", 0, C), V("lu", 0, 28)), ACT.Copy)
+        for s in steps[QPOSS[t]:]:
             s()
         act(V("na"), V("ah", 15, L, 16), ACT.Identity, scale=-1.0)
         act(V("sgn"), V("na"), ACT.Sign)
@@ -332,45 +338,43 @@ def rank_program(g, core, T, topo):
             if k >= 2:
                 s3(k - 2)
         ts(V("ru", nsk, 16), V("so", 127, 128 * nvk, 128), 0.0, ALU.add)
+        for b in range(4):
+            act(V("tt", L * b, L * b + L), pick(plane("pool", b, 0, C + L * t), tl(t)), ACT.Copy)
         if t == 0:
             quant(V("qe"), V("se"), V("eb"))
-            scan(V("sd", 0, L), V("c4"), V("tb", OFF, OFF + L), 0.0, ALU.add, ALU.max)
-            scan(V("sd", L, C), V("c4", 0, C - L), V("tb", OFF + L, OFF + C), 0.0, ALU.add, ALU.max)
-            ts(V("s4"), V("sd", 3, C, 4), 4.0, ALU.mult, col4, ALU.add)
-            tt(V("sums", 0, 4 * C), pick(V("pool", 0, 4 * C), V("s4")), V("xb"), ALU.add)
-            act(V("c16"), V("mm"), ACT.Identity, bias=B, scale=-18 * B)
-        else:
-            act(V("tt"), pick(V("pool", 0, 4 * (C + L * t)), t4(t)), ACT.Copy)
         ts(V("ru", 0, nsk), V("rk", 0, nsk), -16.0, ALU.add)
         new = tops(t + 1)
         op("v", lambda new=new: g.vector.tensor_copy(new[0].indirect(T.ru[:]), T.nf[:]), [V("ru"), V("nf")], [new])
         if t == R - 1:
             dma("y", T.ol[:], T.tb[0:128:16, OFF + C + L * R:OFF + C + L * (R + 1)], [new], [])
-        list4(t4(t + 1), new, "sa")
-        order = (0, 3, 1, 2) if t < R - 1 else (0, 1, 2, 3)
-        for b in order:
+        scan(V("sc"), V("c16"), new, 0.0, ALU.add, ALU.max)
+        ts(tl(t + 1), V("sc", 15, L, 16), b16, ALU.subtract)
+        for b in range(4):
             mx(bank(b), V("qe", 128 * b, 128 * b + 128), V("se", 128 * b, 128 * b + 128), V("ac%d" % t), V("as%d" % t),
                ext=(T.sem["aa%d" % t], arrive) if b == 0 else None)
-        base = 4 * (C + L * t)
-        for b in range(4):
-            if t < R - 1:
-                c = (b + 3) % 4
-                act(V("pool", base + c, base + 4 * L, 4), bank(c), ACT.Copy)
-            tt(V("sums", base + b, base + 4 * L, 4), bank(b), V("tt", b, 4 * L, 4), ALU.add)
-        z, win = "z%d" % (t + 1), V("sums", 0, base + 4 * L)
-        cp(V(z, 0, 2 * L), pick(win, t4(t + 1, 0, 32)))
-        act(V(z, 2 * L, 4 * L), pick(win, t4(t + 1, 32, 64)), ACT.Copy)
-        quant(V("qz%d" % (t + 1)), V("sz%d" % (t + 1)), V(z))
+        base = C + L * t
         if t < R - 1:
-            scan(V("sc"), V("c16"), new, 0.0, ALU.add, ALU.max)
+            for b in range(4):
+                act(plane("pool", b, base, base + L), bank(b), ACT.Copy)
+        for b in range(4):
+            tt(plane("sums", b, base, base + L), bank(b), V("tt", L * b, L * b + L), ALU.add)
+        for b in range(4):
+            read(t + 1, b, "sssv"[b])
+        quant(V("qz%d" % (t + 1)), V("sz%d" % (t + 1)), V("z%d" % (t + 1)))
+        if t == 0:
+            act(tops(0), pick(V("tb", 0, C), tl(0)), ACT.Copy)
+        if t < R - 1:
             ts(V("tw"), V("sc", 15, L, 16), b16, ALU.subtract, float(OFF), ALU.add)
 
-    qz, sz = V("qz%d" % R), V("sz%d" % R)
-    mx(V("psa", 0, L), V("qu"), V("su"), qz, sz)
+    nq, ns = "qz%d" % R, "sz%d" % R
+    qz, sz = V(nq), V(ns)
+    mx(V("psa", 0, 128), V("qu"), V("su"), V(nq, 0, 128), V(ns, 0, 128))
+    mx(V("psb", 0, 128), V("qu"), V("su"), V(nq, 128, L), V(ns, 128, L))
     dma("y", T.oc[:], u8(qz), [qz], [])
     for k in range(4):
-        dma("y" if k < 2 else "s", T.osc[4 * k:4 * k + 4, :], T["sz%d" % R][32 * k:32 * k + 4, :], [sz], [])
-    cp(V("ys"), V("psa", 0, L))
+        dma("y" if k < 3 else "s", T.osc[4 * k:4 * k + 4, :], T[ns][32 * k:32 * k + 4, :], [sz], [])
+    act(V("ys", 0, 128), V("psa", 0, 128), ACT.Copy)
+    cp(V("ys", 128, L), V("psb", 0, 128))
     dma("s", T.y[:], T.ys[:], [V("ys")], [])
 
     hist, known, at, waits = {}, {q: set() for q in queues}, [], []

from concourse.bass import DstId, RemoteDMATransfer
from concourse.mybir import dt, AluOpType, ActivationFunctionType

C, L, R = 448, 256, 3
NODES = C + L * R
PW = NODES - L
OFF = NODES
B = 2048.0
NVKS = (10, 10, 10)
PRE = (4, 1, 1)
NVAS = (1, 0, 0)
QPOSS = (0, 3, 3)
NVM, NSM = max(NVKS), 16 - min(NVKS)
SGW = L + 2

Q4 = "float8_e4m3fn_x4"
WIDTHS = {
    "bfloat16": {"pool": 4 * PW, "sums": 4 * NODES, "xs": 4 * C, "ub": 512, "eb": 2048, "ones": 128, "mm": L, "nm": L, "tt": 4 * L,
                 "eq": L, "ncr": L, "fl": NVM * L, "so": NVM * 128},
    "float32": {"tb": OFF + C + 4 * L, "rf": 8, "j16": L, "c16": L, "cw0": 48, "cw": 48,
                "sc": L, "nf": L, "tw": 16, "prod": L, "ah": L, "na": 16, "sgn": 16, "i1": 16, "i2": 16, "sg": NSM * SGW,
                "junk": NSM * SGW, "rk": 16, "ys": L},
    "int32": {"li": 44, "pc": 1, "ri": 1, "uo": 8},
    "uint16": {"lu": 44, "uu": 8, "tl": 16 * R, "iu": 16, "ru": 16},
    Q4: {"qu": 128, "qr": 128, "wq": 512, "qe": 512},
    "uint8": {"su": 128, "sr": 128, "wp": 512, "se": 512},
}
for _t in range(R + 1):
    WIDTHS["bfloat16"]["z%d" % _t] = 4 * L
    WIDTHS[Q4]["qz%d" % _t] = L
    WIDTHS["uint8"]["sz%d" % _t] = L
for _t in range(R):
    WIDTHS["bfloat16"]["h%d" % _t] = 4 * L
    for _a, _b in (("qh", "sh"), ("rc", "rs"), ("ac", "as")):
        WIDTHS[Q4]["%s%d" % (_a, _t)] = L
        WIDTHS["uint8"]["%s%d" % (_b, _t)] = L
SCRATCH = {_n: ("sbuf", [128, _w], _d) for _d in WIDTHS for _n, _w in WIDTHS[_d].items()}
for _n, _w in (("psa", 512), ("psb", 512), ("psh", 2048)):
    SCRATCH[_n] = ("psum", [128, _w], "float32")

POOLS = {"v": 56, "s": 40, "t": 14, "g": 12, "d": 16}
SEMAPHORES = [q + str(i) for q in POOLS for i in range(POOLS[q])] + ["ls"] + ["ra%d" % t for t in range(R)] + ["aa%d" % t for t in range(R)]

ALU, ACT = AluOpType, ActivationFunctionType


def bits(es):
    m = 0
    for e in es:
        m |= 1 << e
    return m


def route(T, topo, r):
    src, dst = T.cores[r], T.cores[(r + 1) % len(T.cores)]
    if topo.may_write(src, dst):
        return None
    ok = [c for c in topo.cores_of(src) if c != src and topo.may_write(c, dst)]
    near = [c for c in ok if topo.die(c) == topo.die(src)]
    far = [c for c in ok if topo.die(c) != topo.die(src)]
    return [near[0], far[0], near[1]]


def relay_program(g, core, T, topo):
    n = len(T.cores)
    for r in range(n):
        way = route(T, topo, r)
        if way is None or core not in way:
            continue
        src, dst = T.cores[r], T.cores[(r + 1) % n]
        k = way.index(core)
        on = len(topo.engines(src, core))
        rid, pid = topo.addr(dst, core)
        mask = topo.mask(core, dst)
        for t in range(R):
            if k < 2:
                g.wait_ge(T.sem["ra%d" % t], on // 2)
                a, b = 128 * k, 128 * k + 128
                g.remote_dma(T["ac%d" % t][:, a:b].bitcast(dt.uint8), T["rc%d" % t][:, a:b].bitcast(dt.uint8),
                             T.sem["aa%d" % t], T.sem.ls, pid, rid, mask)
            else:
                g.wait_ge(T.sem["ra%d" % t], on)
                g.remote_dma(T["as%d" % t][:], T["rs%d" % t][:], T.sem["aa%d" % t], T.sem.ls, pid, rid, mask)
        g.wait_ge(T.sem.ls, R * len(topo.engines(core, dst)))


def rank_program(g, core, T, topo):
    rank = T.rank_of(core)
    if rank is None:
        relay_program(g, core, T, topo)
        return
    n = len(T.cores)
    nxt, prv = T.cores[(rank + 1) % n], T.cores[(rank - 1) % n]
    way, back = route(T, topo, rank), route(T, topo, (rank - 1) % n)
    if back is None:
        arrive = 2 * len(topo.engines(prv, core))
    else:
        arrive = sum(len(topo.engines(c, core)) for c in back)
    queues = {"v": g.vector, "s": g.scalar, "t": g.tensor, "g": g, "y": g.sync}
    ops = []

    def V(name, a=None, b=None, s=1):
        w = T[name].shape[1]
        a, b = (0 if a is None else a), (w if b is None else b)
        ap = T[name][:, a:b] if s == 1 else T[name][:, a:b:s]
        if SCRATCH[name][0] == "psum":
            return (ap, [(name, 1 << (a // 512))])
        return (ap, [(name, bits(range(a, b, s)))])

    def pick(win, off):
        return (win[0].indirect(off[0]), win[1] + off[1])

    def op(q, fn, reads, writes, ext=None, kind="c"):
        ops.append({"q": q, "fn": fn, "r": [x for v in reads for x in v[1]], "w": [x for v in writes for x in v[1]], "ext": ext, "kind": kind})

    def sc(x):
        return (x[0], [x]) if isinstance(x, tuple) else (x, [])

    def ts(out, in0, s1, o0, s2=None, o1=None):
        (a, ra), (b, rb) = sc(s1), sc(s2)
        if o1 is None:
            op("v", lambda: g.vector.tensor_scalar(out[0], in0[0], a, None, o0), [in0] + ra, [out])
        else:
            op("v", lambda: g.vector.tensor_scalar(out[0], in0[0], a, b, o0, o1), [in0] + ra + rb, [out])

    def tt(out, in0, in1, o):
        op("v", lambda: g.vector.tensor_tensor(out[0], in0[0], in1[0], o), [in0, in1], [out])

    def cp(out, in_):
        op("v", lambda: g.vector.tensor_copy(out[0], in_[0]), [in_], [out])

    def scan(out, d0, d1, init, o0, o1):
        a, ra = sc(init)
        op("v", lambda: g.vector.tensor_tensor_scan(out[0], d0[0], d1[0], a, o0, o1), [d0, d1] + ra, [out])

    def act(out, in_, f, bias=None, scale=None, acc=None):
        kw, rd, wr = {}, [in_], [out]
        if bias is not None:
            kw["bias"], ra = sc(bias)
            rd += ra
        if scale is not None:
            kw["scale"] = scale
        if acc is not None:
            kw["accum_out"] = acc[0]
            wr.append(acc)
        op("s", lambda: g.scalar.activation(out[0], in_[0], f, **kw), rd, wr)

    def quant(q, s, in_):
        op("v", lambda: g.vector.quantize_mx(q[0], s[0], in_[0]), [in_], [q, s])

    def mx(out, lq, ls, rq, rs, ext=None):
        op("t", lambda: g.tensor.matmul_mx(out[0], lq[0], ls[0], rq[0], rs[0], True, True), [lq, ls, rq, rs], [out], ext)

    def iota(out, pattern, base, cm, fl=True):
        if fl:
            op("g", lambda: g.iota(out[0], pattern, base, cm, allow_small_or_imprecise_dtypes=True), [], [out])
        else:
            op("g", lambda: g.iota(out[0], pattern, base, cm), [], [out])

    def dma(q, out, in_, reads, writes):
        op(q, lambda: queues[q].dma_start(out, in_), reads, writes, kind="d")

    def u8(v):
        return v[0].bitcast(dt.uint8)

    rcol, b16, negr = [V("rf", i, i + 1) for i in range(3)]

    dma("y", T.li[:, 0:28], T.par[:], [], [V("li", 0, 28)])
    dma("y", T.li[:, 28:44], T.top[:], [], [V("li", 28, 44)])
    dma("s", T.xs[:], T.x[:], [], [V("xs")])
    dma("y", u8(V("wq")), T.wc[:], [V("li", 28, 44)], [V("wq")])
    dma("y", T.wp[:], T.ws[:], [], [V("wp")])
    dma("y", T.ub[:], T.u[:], [], [V("ub")])

    iota(V("pc"), [[0, 1]], 0, 1, False)
    iota(V("j16"), [[0, 16], [1, 16]], 0, 0)
    iota(V("uo"), [[16, 8]], 0, 0, False)
    op("v", lambda: g.vector.memset(T.ones[:], 1.0), [], [V("ones")])
    op("v", lambda: g.vector.memset(T.eb[:], 0.0), [], [V("eb")])

    def unit(b):
        o = V("eb", 512 * b + b, 512 * b + 512, 4)
        op("g", lambda: g.affine_select(o[0], T.ones[:], [[-1, 128]], ALU.is_equal, 0.0, 0, 1), [V("ones")], [o])
    iota(V("tb", 0, C), [[1, C]], 0, 0)
    for b in range(4):
        unit(b)
    iota(V("cw0"), [[16, 48]], C, 0)
    iota(V("tb", C, NODES), [[1, NODES - C]], C, 0)

    ts(V("ri"), V("pc"), 15, ALU.bitwise_and)
    cp(rcol, V("ri"))
    cp(V("uu"), V("uo"))
    act(negr, rcol, ACT.Identity, scale=-1.0)
    act(b16, rcol, ACT.Identity, bias=15 * B, scale=-B)
    act(V("prod"), V("j16"), ACT.Abs, bias=negr)
    act(V("mm"), V("prod"), ACT.Relu, bias=1.0, scale=-1.0)

    def tops(t):
        return V("tb", OFF + C + L * t, OFF + C + L * (t + 1))

    def tl(t, a=0, b=16):
        return V("lu", 28 + a, 28 + b) if t == 0 else V("tl", 16 * (t - 1) + a, 16 * (t - 1) + b)

    def plane(name, b, lo, hi):
        w = PW if name == "pool" else NODES
        return V(name, w * b + lo, w * b + hi)

    def read(t, b, eng, a=0, e=16):
        o, i = V("z%d" % t, 64 * a + b, 64 * e, 4), pick(plane("sums", b, 0, C + L * t), tl(t, a, e))
        if eng == "v":
            cp(o, i)
        else:
            act(o, i, ACT.Copy)

    cp(plane("pool", 0, 0, C), V("xs", 0, 4 * C, 4))
    cp(V("lu"), V("li"))
    for b in range(1, 4):
        act(plane("pool", b, 0, C), V("xs", b, 4 * C, 4), ACT.Copy)
    for b in range(4):
        tt(plane("sums", b, 0, C), pick(plane("pool", b, 0, C), V("lu", 0, 28)), V("xs", b, 4 * C, 4), ALU.add)
        if b < 3:
            read(0, b, "s")
        if b == 1:
            act(V("nm"), V("prod"), ACT.Sign)
        if b == 2:
            act(V("c16"), V("mm"), ACT.Identity, bias=B, scale=-18 * B)
    read(0, 3, "v", 0, 8)
    read(0, 3, "s", 8, 16)
    quant(V("qz0"), V("sz0"), V("z0"))
    quant(V("qu"), V("su"), V("ub"))
    op("v", lambda: g.vector.tensor_copy(T.qr[:].bitcast(dt.uint32), T.qu[:].bitcast(dt.uint32).indirect(T.uu[:])), [V("qu"), V("uu")], [V("qr")])
    cp(V("sr"), pick(V("su"), V("uu")))
    sent = [0]

    def send(t):
        qh, sh = "qh%d" % t, "sh%d" % t
        if way is None:
            rid, pid = topo.addr(nxt, core)
            mask = topo.mask(core, nxt)
            op("g", lambda: g.remote_dma(u8(V("ac%d" % t)), u8(V(qh)), T.sem["aa%d" % t], T.sem.ls, pid, rid, mask), [V(qh)], [], kind="r")
            op("g", lambda: g.remote_dma(T["as%d" % t][:], T[sh][:], T.sem["aa%d" % t], T.sem.ls, pid, rid, mask), [V(sh)], [], kind="r")
            sent[0] += 2 * len(topo.engines(core, nxt))
            return
        parts = []
        for k in range(2):
            es = topo.engines(core, way[k])[k::2]
            rid, pid = topo.addr(way[k], core)
            parts.append(RemoteDMATransfer(dst_ids=[DstId(rid=rid, pnc=pid)], dma_engine_mask=bits(es), remote_sem=T.sem["ra%d" % t],
                                           src=u8(V(qh, 128 * k, 128 * k + 128)), dst=u8(V("rc%d" % t, 128 * k, 128 * k + 128))))
            sent[0] += len(es)
        op("g", lambda: g.remote_dma_fused(parts, local_sem=T.sem.ls), [V(qh)], [], kind="r")
        rid, pid = topo.addr(way[2], core)
        mask = topo.mask(core, way[2])
        op("g", lambda: g.remote_dma(T["rs%d" % t][:], T[sh][:], T.sem["ra%d" % t], T.sem.ls, pid, rid, mask), [V(sh)], [], kind="r")
        sent[0] += len(topo.engines(core, way[2]))

    for t in range(R):
        qz, sz, h = V("qz%d" % t), V("sz%d" % t), "h%d" % t
        sa, sb = V("psa", 0, L), V("psb", 0, L)
        nvk = NVKS[t]
        nsk = 16 - nvk

        def bank(b):
            return V("psh", 512 * b, 512 * b + L)

        def wmx(b):
            mx(bank(b), V("wq", 128 * b, 128 * b + 128), V("wp", 128 * b, 128 * b + 128), qz, sz)
        for b in range(PRE[t]):
            wmx(b)
        mx(sa, V("qr"), V("sr"), qz, sz)
        for b in range(PRE[t], 4):
            wmx(b)
        mx(sb, V("qr"), V("sr"), qz, sz)
        for b in range(4):
            if b >= 4 - NVAS[t]:
                ts(V(h, b, 4 * L, 4), bank(b), 0.0, ALU.max, 0.015625, ALU.mult)
            else:
                act(V(h, b, 4 * L, 4), bank(b), ACT.Relu, scale=0.015625)
        steps = [lambda: tt(V("prod"), sa, V("mm"), ALU.mult),
                 lambda: scan(V("ah"), V("nm"), V("prod"), 0.0, ALU.mult, ALU.add),
                 lambda: tt(V("eq"), sa, V("ah"), ALU.is_equal),
                 lambda: scan(V("ncr"), V("nm"), V("eq"), 0.0, ALU.mult, ALU.subtract)]
        for s in steps[:QPOSS[t]]:
            s()
        quant(V("qh%d" % t), V("sh%d" % t), V(h))
        send(t)
        if t == 0:
            act(V("tb", OFF, OFF + C), pick(V("tb", 0, C), V("lu", 0, 28)), ACT.Copy)
        for s in steps[QPOSS[t]:]:
            s()
        act(V("na"), V("ah", 15, L, 16), ACT.Identity, scale=-1.0)
        act(V("sgn"), V("na"), ACT.Sign)
        if t == 0:
            ts(V("tw"), V("li", 28, 44), float(OFF), ALU.add)
            ts(V("cw"), V("cw0"), rcol, ALU.add)

        def vcmp(i):
            e = 16 * (nsk + i) + 16
            a = V("ah", e - 1, e)
            ts(V("fl", L * i, L * i + e), V("psa", 0, e), a, ALU.is_ge)
            if e < L:
                ts(V("fl", L * i + e, L * i + L), V("psa", e, L), a, ALU.is_gt)

        def vsum(i):
            e = 16 * (nsk + i) + 16
            scan(V("so", 128 * i, 128 * i + 128), V("fl", L * i, L * i + 128), V("fl", L * i + 128, L * i + L), V("ncr", e - 1, e), ALU.add, ALU.add)

        def s1(k):
            act(V("sg", SGW * k, SGW * k + L), sb, ACT.Sign, bias=V("na", k, k + 1))

        def s2(k):
            o, e = SGW * k, 16 * k + 16
            act(V("junk", o, o + e), V("sg", o, o + e), ACT.Sign, bias=1.0, acc=V("sg", o + L, o + L + 1))

        def s3(k):
            o, e = SGW * k, 16 * k + 16
            act(V("junk", o + e, o + SGW), V("sg", o + e, o + SGW), ACT.Relu, acc=V("rk", k, k + 1))

        vcmp(0)
        tt(V("i1"), V("sgn"), V("tw"), ALU.mult)
        vcmp(1)
        tt(V("i2"), V("i1"), V("cw", 16 * t, 16 * t + 16), ALU.max)
        vsum(0)
        cp(V("iu"), V("i2"))
        for i in range(2, nvk):
            vcmp(i)
            vsum(i - 1)
        vsum(nvk - 1)
        for k in range(nsk + 2):
            if k < nsk:
                s1(k)
            if k == 1:
                act(V("sg", SGW - 1, nsk * SGW, SGW), V("ncr", 15, 16 * nsk, 16), ACT.Identity, bias=16.0)
            if 1 <= k <= nsk:
                s2(k - 1)
            if k == nsk:
                act(V("nf"), pick(V("tb", 0, OFF + C + L * t), V("iu")), ACT.Copy)
            if k >= 2:
                s3(k - 2)
        ts(V("ru", nsk, 16), V("so", 127, 128 * nvk, 128), 0.0, ALU.add)
        for b in range(4):
            act(V("tt", L * b, L * b + L), pick(plane("pool", b, 0, C + L * t), tl(t)), ACT.Copy)
        if t == 0:
            quant(V("qe"), V("se"), V("eb"))
        ts(V("ru", 0, nsk), V("rk", 0, nsk), -16.0, ALU.add)
        new = tops(t + 1)
        op("v", lambda new=new: g.vector.tensor_copy(new[0].indirect(T.ru[:]), T.nf[:]), [V("ru"), V("nf")], [new])
        if t == R - 1:
            dma("y", T.ol[:], T.tb[0:128:16, OFF + C + L * R:OFF + C + L * (R + 1)], [new], [])
        scan(V("sc"), V("c16"), new, 0.0, ALU.add, ALU.max)
        ts(tl(t + 1), V("sc", 15, L, 16), b16, ALU.subtract)
        for b in range(4):
            mx(bank(b), V("qe", 128 * b, 128 * b + 128), V("se", 128 * b, 128 * b + 128), V("ac%d" % t), V("as%d" % t),
               ext=(T.sem["aa%d" % t], arrive) if b == 0 else None)
        base = C + L * t
        if t < R - 1:
            for b in range(4):
                act(plane("pool", b, base, base + L), bank(b), ACT.Copy)
        for b in range(4):
            tt(plane("sums", b, base, base + L), bank(b), V("tt", L * b, L * b + L), ALU.add)
        for b in range(4):
            read(t + 1, b, "sssv"[b])
        quant(V("qz%d" % (t + 1)), V("sz%d" % (t + 1)), V("z%d" % (t + 1)))
        if t == 0:
            act(tops(0), pick(V("tb", 0, C), tl(0)), ACT.Copy)
        if t < R - 1:
            ts(V("tw"), V("sc", 15, L, 16), b16, ALU.subtract, float(OFF), ALU.add)

    nq, ns = "qz%d" % R, "sz%d" % R
    qz, sz = V(nq), V(ns)
    mx(V("psa", 0, 128), V("qu"), V("su"), V(nq, 0, 128), V(ns, 0, 128))
    mx(V("psb", 0, 128), V("qu"), V("su"), V(nq, 128, L), V(ns, 128, L))
    dma("y", T.oc[:], u8(qz), [qz], [])
    for k in range(4):
        dma("y" if k < 3 else "s", T.osc[4 * k:4 * k + 4, :], T[ns][32 * k:32 * k + 4, :], [sz], [])
    act(V("ys", 0, 128), V("psa", 0, 128), ACT.Copy)
    cp(V("ys", 128, L), V("psb", 0, 128))
    dma("s", T.y[:], T.ys[:], [V("ys")], [])

    hist, known, at, waits = {}, {q: set() for q in queues}, [], []
    for i, o in enumerate(ops):
        deps = set()
        accs = [(x, False) for x in o["r"]] + [(x, True) for x in o["w"]]
        for acc, wr in accs:
            psum = SCRATCH[acc[0]][0] == "psum"
            for j, m, w in hist.get(acc[0], []):
                if m & acc[1] and (w or wr or (psum and ops[j]["q"] != o["q"])):
                    deps.add(j)
        mine = []
        for j in sorted(deps, reverse=True):
            if j not in known[o["q"]]:
                mine.append(j)
                known[o["q"]] |= at[j] | {j}
        waits.append(mine)
        at.append(set(known[o["q"]]))
        for acc, wr in accs:
            hist.setdefault(acc[0], []).append((i, acc[1], wr))
    waiters = {}
    for i, w in enumerate(waits):
        for j in w:
            waiters.setdefault(j, []).append(i)
    group = {}
    for j, w in waiters.items():
        group[j] = (ops[j]["q"], tuple(w)) if ops[j]["kind"] == "c" else ("own", j)
    members = {}
    for j in sorted(group):
        members.setdefault(group[j], []).append(j)
    used, last, count, mark = {q: 0 for q in POOLS}, {}, {}, {}
    for i, o in enumerate(ops):
        q = queues[o["q"]]
        done = []
        for j in waits[i]:
            if group[j] not in done:
                done.append(group[j])
                q.wait_ge(*mark[group[j]])
        if o["ext"] is not None:
            q.wait_ge(*o["ext"])
        if o["kind"] == "d":
            name = "d%d" % used["d"]
            used["d"] += 1
            mark[("own", i)] = (T.sem[name], 16)
            o["fn"]().then_inc(T.sem[name], 16)
        elif i in group:
            k = group[i]
            if k not in mark:
                name = o["q"] + str(used[o["q"]] % POOLS[o["q"]])
                used[o["q"]] += 1
                if name in last and any(j not in at[i] for j in members[last[name]]):
                    q.wait_ge(*mark[last[name]])
                last[name] = k
                count[name] = count.get(name, 0) + len(members[k])
                mark[k] = (T.sem[name], count[name])
            o["fn"]().then_inc(mark[k][0], 1)
        else:
            o["fn"]()
    for i, o in enumerate(ops):
        if o["kind"] == "d" and i not in group:
            queues[o["q"]].wait_ge(*mark[("own", i)])
    g.wait_ge(T.sem.ls, sent[0])
